import numpy as np
import ml_dtypes


def mxq(x, axis, fmt="e4m3"):
    dtype, down = {"e4m3": (ml_dtypes.float8_e4m3fn, 7), "e5m2": (ml_dtypes.float8_e5m2, 14)}[fmt]
    v = np.moveaxis(np.asarray(x, np.float32).astype(ml_dtypes.bfloat16).astype(np.float64), axis, -1)
    blocks = v.reshape(v.shape[:-1] + (-1, 32))
    amax = np.abs(blocks).max(-1, keepdims=True)
    byte = np.maximum(np.where(amax > 0, np.frexp(amax)[1] - 1 + 127, 0) - down, 1)
    scale = np.exp2(byte - 127.0)
    codes = (blocks / scale).astype(np.float32).astype(dtype).astype(np.float64)
    return np.moveaxis((codes * scale).reshape(v.shape), -1, axis)


WIDE = False


def mx_kscale(k):
    if not WIDE:
        return np.ones(k)
    levels = np.array([30, -30])
    if k % 512:
        return np.exp2(np.random.permutation(np.resize(levels, k // 32))).repeat(32)
    a = np.empty((k // 512, 16))
    for p in range(k // 512):
        a[p, :8] = np.random.permutation(np.resize(levels, 8))
        for g in range(8):
            far = levels[np.abs(levels - a[p, g]) >= 10]
            a[p, g + 8] = far[np.random.randint(len(far))]
    return np.exp2(a.ravel()).repeat(32)


def f64(x):
    return np.asarray(x).astype(np.float64)


def striped(idx):
    return np.tile(np.asarray(idx).reshape(-1, 16).T, (8, 1)).astype(np.uint16)


def unstriped(offs):
    return offs[:16].T.reshape(-1).astype(np.int64)


E2M1 = np.array([0.0, 0.5, 1.0, 1.5, 2.0, 3.0, 4.0, 6.0, -0.0, -0.5, -1.0, -1.5, -2.0, -3.0, -4.0, -6.0])


def pack_weight(w, fmt):
    k, n = w.shape
    w = f64(np.asarray(w, np.float32).astype(ml_dtypes.bfloat16)).reshape(k // 32, 32, n)
    amax = np.abs(w).max(1)
    if fmt in ("e4m3", "e5m2"):
        byte = np.frexp(amax)[1] - 1 + 127 - (7 if fmt == "e4m3" else 14)
    else:
        mant, ex = np.frexp(amax / 6.0)
        byte = np.where(mant > 0.5, ex, ex - 1) + 127
    byte = np.clip(np.where(amax > 0, byte, 1), 1, 254)
    scaled = (w * np.exp2(127.0 - byte)[:, None, :]).reshape(k, n).astype(np.float32)
    by_word = np.ascontiguousarray(scaled.reshape(k // 512, 128, 4, n).transpose(0, 1, 3, 2))
    if fmt in ("e4m3", "e5m2"):
        words = by_word.astype(ml_dtypes.float8_e4m3fn if fmt == "e4m3" else ml_dtypes.float8_e5m2).view(np.uint8)
    else:
        c = by_word.astype(ml_dtypes.float4_e2m1fn).view(np.uint8) & 0xF
        words = (c[..., 0::2] | (c[..., 1::2] << 4)).reshape(k // 512, 128, 2 * n)
    return np.ascontiguousarray(words), np.ascontiguousarray(byte.astype(np.uint8).reshape(k // 512, 16, n))


def unpack_weight(words, scales, fmt):
    g, _, n = scales.shape
    words = np.ascontiguousarray(words).reshape(g, 128, n, -1)
    if fmt in ("e4m3", "e5m2"):
        vals = words.view(ml_dtypes.float8_e4m3fn if fmt == "e4m3" else ml_dtypes.float8_e5m2).astype(np.float64)
    else:
        nib = np.empty((g, 128, n, 4), np.uint8)
        nib[..., 0::2] = words & 0xF
        nib[..., 1::2] = words >> 4
        vals = E2M1[nib]
    vals = vals * np.repeat(np.exp2(scales.astype(np.float64) - 127.0), 8, axis=1)[..., None]
    return vals.transpose(0, 1, 3, 2).reshape(g * 512, n)


K, T, Z, J, R, C, N, E = 512, 1024, 1024, 256, 512, 512, 256, 1024


def setup_inputs():
    n = np.random.standard_normal
    idx = np.random.permutation(T)[:J]
    idx2 = np.random.permutation(Z)[:J]
    idx3 = np.random.permutation(C)[:J]
    idx4 = np.random.permutation(C)[:J]
    idx5 = np.random.permutation(E)[:J]
    fk = mx_kscale(K)
    fr = mx_kscale(R)
    xtp = pack_weight(n((K, T)) / fk[:, None], "e5m2")
    xop = pack_weight(n((K, Z)) / fk[:, None], "e4m3")
    wp = pack_weight(n((K, R)) * 1 / np.sqrt(K) * fk[:, None] * fr, "e2m1")
    wbp = pack_weight(n((R, N)) * 1 / np.sqrt(R) / fr[:, None], "e2m1")
    return {
        "xt_words": xtp[0],
        "xt_scales": xtp[1],
        "xo_words": xop[0],
        "xo_scales": xop[1],
        "w_words": wp[0],
        "w_scales": wp[1],
        "wb_words": wbp[0],
        "wb_scales": wbp[1],
        "tz": (n((N, E))).astype(np.float32),
        "offs": striped(idx),
        "offs2": striped(idx2),
        "offs3": striped(idx3),
        "offs4": striped(idx4),
        "offs5": striped(idx5),
    }


def reference(xt_words, xt_scales, xo_words, xo_scales, w_words, w_scales, wb_words, wb_scales, tz, offs, offs2, offs3, offs4, offs5):
    idx = unstriped(offs)
    idx2 = unstriped(offs2)
    idx3 = unstriped(offs3)
    idx4 = unstriped(offs4)
    idx5 = unstriped(offs5)
    xtu = unpack_weight(xt_words, xt_scales, "e5m2")
    xou = unpack_weight(xo_words, xo_scales, "e4m3")
    wu = unpack_weight(w_words, w_scales, "e2m1")
    wbu = unpack_weight(wb_words, wb_scales, "e2m1")
    xtidxg = xtu[:, idx]
    a = wu.T @ xtidxg
    xoidx2g = xou[:, idx2]
    b = wu.T @ xoidx2g
    pw = np.zeros((R, C))
    pw[:, idx3] = a
    hid = np.maximum(pw[:, idx4], b)
    hidq = mxq(hid, 0, "e4m3")
    p = wbu.T @ hidq
    y = p + f64(tz)[:, idx5]
    return y

@@ -1,0 +1,186 @@
+from contextlib import ExitStack
+
+import concourse.mybir as mybir
+
+K, T, Z, J, R, C, N, E = 512, 1024, 1024, 256, 512, 512, 256, 1024
+FLOPS = 2 * (2 * K * R * J + R * N * J)
+
+F32 = mybir.dt.float32
+BF16 = mybir.dt.bfloat16
+I32 = mybir.dt.int32
+U32 = mybir.dt.uint32
+U16 = mybir.dt.uint16
+U8 = mybir.dt.uint8
+E4M3 = mybir.dt.float8_e4m3fn_x4
+E5M2 = mybir.dt.float8_e5m2_x4
+E2M1 = mybir.dt.float4_e2m1fn_x4
+COPY = mybir.ActivationFunctionType.Copy
+MAX = mybir.AluOpType.max
+ADD = mybir.AluOpType.add
+
+P = 128
+PACK = 4
+HALF = J // 2
+LIST_COLS = J // 16
+
+
+def tile_list_oneforboth_board_one_tabled_kernel(
+    tc, xt_words, xt_scales, xo_words, xo_scales, w_words, w_scales, wb_words, wb_scales, tz,
+    offs, offs2, offs3, offs4, offs5, out,
+):
+    nc = tc.nc
+    with ExitStack() as ctx:
+        lists = ctx.enter_context(tc.tile_pool(name="lists", bufs=1))
+        sb = ctx.enter_context(tc.tile_pool(name="sb", bufs=1))
+        ps = ctx.enter_context(tc.psum_pool(name="ps", bufs=1))
+
+        idx = lists.tile([P, LIST_COLS], U16, name="idx")
+        idx2 = lists.tile([P, LIST_COLS], U16, name="idx2")
+        idx3 = lists.tile([P, LIST_COLS], U16, name="idx3")
+        idx4 = lists.tile([P, LIST_COLS], U16, name="idx4")
+        idx5 = lists.tile([P, LIST_COLS], U16, name="idx5")
+
+        xt_w = sb.tile([P, T], I32, name="xt_w", align_bytes=64)
+        xt_s = sb.tile([P, T], U8, name="xt_s", align_bytes=64)
+        xo_w = sb.tile([P, Z], I32, name="xo_w", align_bytes=64)
+        xo_s = sb.tile([P, Z], U8, name="xo_s", align_bytes=64)
+        w_raw = sb.tile([P, 2 * R], U8, name="w_raw", align_bytes=64)
+        ws_raw = sb.tile([P, R], U8, name="ws_raw", align_bytes=64)
+        w_q = sb.tile([P, 2 * R], U8, name="w_q", align_bytes=64)
+        w_s = sb.tile([P, R], U8, name="w_s", align_bytes=64)
+        wb_q = sb.tile([P, 2 * N], U8, name="wb_q", align_bytes=64)
+        wb_s = sb.tile([P, N], U8, name="wb_s", align_bytes=64)
+        tz_sb = sb.tile([P, 2, E], F32, name="tz_sb", align_bytes=64)
+        board = [sb.tile([P, C], F32, name="board%d" % t, align_bytes=64) for t in range(PACK)]
+
+        def load_rows(queue, plane, scales, q):
+            rows = scales[0, 4 * q : 4 * q + 4, :].bitcast(I32)
+            queue.dma_start(plane[32 * q : 32 * q + 32, :].bitcast(I32), rows.partition_broadcast(8))
+
+        for t in range(PACK):
+            nc.vector.memset(board[t][:], 0.0)
+
+        for q in range(4):
+            load_rows(nc.sync if q < 2 else nc.scalar, xt_s, xt_scales, q)
+        nc.sync.dma_start(xt_w[:], xt_words[0].rearrange("p n t -> p (n t)").bitcast(I32))
+        nc.sync.dma_start(idx[:], offs)
+        nc.sync.dma_start(w_raw[:].bitcast(I32), w_words[0].bitcast(I32))
+        nc.sync.dma_start(xo_w[:], xo_words[0].rearrange("p n t -> p (n t)").bitcast(I32))
+        for q in range(4):
+            load_rows(nc.sync, ws_raw, w_scales, q)
+        nc.sync.dma_start(idx2[:], offs2)
+        nc.sync.dma_start(idx3[:], offs3)
+        for q in range(4):
+            load_rows(nc.sync if q < 1 else nc.gpsimd, xo_s, xo_scales, q)
+        nc.sync.dma_start(idx4[:], offs4)
+        nc.sync.dma_start(tz_sb[:], tz.rearrange("(m p) e -> p m e", p=P))
+        nc.sync.dma_start(wb_q[:].bitcast(I32), wb_words[0].bitcast(I32))
+        for q in range(4):
+            load_rows(nc.sync, wb_s, wb_scales, q)
+        nc.sync.dma_start(idx5[:], offs5)
+
+        xt_gw = sb.tile([P, J], U32, name="xt_gw", align_bytes=64)
+        xt_gs = sb.tile([P, J], U8, name="xt_gs", align_bytes=64)
+        xo_gw = sb.tile([P, J], U32, name="xo_gw", align_bytes=64)
+        xo_gs = sb.tile([P, J], U8, name="xo_gs", align_bytes=64)
+        nc.vector.tensor_copy(
+            w_q[:].bitcast(U16).rearrange("p (t m) -> p t m", t=PACK),
+            w_raw[:].bitcast(U16).rearrange("p (m t) -> p t m", t=PACK),
+        )
+        nc.vector.tensor_copy(xt_gw[:], xt_w[:].bitcast(U32).indirect(idx[:]))
+        nc.vector.tensor_copy(xt_gs[:], xt_s[:].indirect(idx[:]))
+        nc.vector.tensor_copy(
+            w_s[:].rearrange("p (t m) -> p t m", t=PACK),
+            ws_raw[:].rearrange("p (m t) -> p t m", t=PACK),
+        )
+        nc.vector.tensor_copy(xo_gw[:], xo_w[:].bitcast(U32).indirect(idx2[:]))
+        nc.vector.tensor_copy(xo_gs[:], xo_s[:].indirect(idx2[:]))
+
+        def w_slice(t):
+            return dict(lhsT=w_q[:, 2 * P * t : 2 * P * (t + 1)].bitcast(E2M1), lhsT_scale=w_s[:, P * t : P * (t + 1)])
+
+        a_ps = [ps.tile([P, J], F32, name="a_ps%d" % t) for t in range(PACK)]
+        a_sb = [sb.tile([P, J], F32, name="a_sb%d" % t, tag="stage%d" % t, align_bytes=64) for t in range(PACK)]
+        for t in range(PACK):
+            nc.tensor.matmul_mx(
+                out=a_ps[t][:], rhs=xt_gw[:].bitcast(E5M2), rhs_scale=xt_gs[:], start=True, stop=True, **w_slice(t)
+            )
+
+        for t in range(PACK):
+            nc.scalar.activation(a_sb[t][:], a_ps[t][:], COPY)
+        for t in (0, 1):
+            nc.vector.tensor_copy(board[t][:].indirect(idx3[:]), a_sb[t][:])
+        for t in (2, 3):
+            nc.scalar.activation(board[t][:].indirect(idx3[:]), a_sb[t][:], COPY)
+
+        b_ps = [ps.tile([P, PACK, HALF], F32, name="b_ps%d" % h) for h in range(2)]
+        for h in range(2):
+            cols = slice(HALF * h, HALF * (h + 1))
+            for t in range(PACK):
+                nc.tensor.matmul_mx(
+                    out=b_ps[h][:, t, :], rhs=xo_gw[:, cols].bitcast(E4M3), rhs_scale=xo_gs[:, cols],
+                    start=True, stop=True, **w_slice(t)
+                )
+
+        read = [sb.tile([P, PACK, HALF], F32, name="read%d" % h, align_bytes=64) for h in range(2)]
+        hid = [sb.tile([P, HALF, PACK], BF16, name="hid%d" % h, align_bytes=64) for h in range(2)]
+        hid_q = [sb.tile([P, HALF], U32, name="hid_q%d" % h, align_bytes=64) for h in range(2)]
+        hid_s = [sb.tile([P, HALF], U8, name="hid_s%d" % h, align_bytes=64) for h in range(2)]
+        tz_g = sb.tile([P, 2, 2, HALF], F32, name="tz_g", tag="stage3", align_bytes=64)
+        p_ps = [ps.tile([P, 2, HALF], F32, name="p_ps%d" % h) for h in range(2)]
+        res = [sb.tile([P, 2, HALF], F32, name="res%d" % h, align_bytes=64) for h in range(2)]
+        out_v = out.rearrange("(m p) j -> p m j", p=P)
+
+        def half_list(lst, h):
+            return lst[:, (LIST_COLS // 2) * h : (LIST_COLS // 2) * (h + 1)]
+
+        def look_up(on_vector, h, t):
+            window = board[t][:].indirect(half_list(idx4, h))
+            if on_vector:
+                nc.vector.tensor_copy(read[h][:, t, :], window)
+            else:
+                nc.scalar.activation(read[h][:, t, :], window, COPY)
+
+        def larger(h):
+            nc.vector.tensor_tensor(
+                hid[h][:].rearrange("p (c i) t -> p c t i", i=4),
+                read[h][:].rearrange("p t (c i) -> p c t i", i=4),
+                b_ps[h][:].rearrange("p t (c i) -> p c t i", i=4),
+                MAX,
+            )
+
+        def quantise(h):
+            nc.vector.quantize_mx(
+                out=hid_q[h][:].bitcast(E4M3), scales=hid_s[h][:], in_=hid[h][:].rearrange("p j t -> p (j t)")
+            )
+            for m in range(2):
+                nc.tensor.matmul_mx(
+                    out=p_ps[h][:, m, :],
+                    lhsT=wb_q[:, 2 * P * m : 2 * P * (m + 1)].bitcast(E2M1), lhsT_scale=wb_s[:, P * m : P * (m + 1)],
+                    rhs=hid_q[h][:].bitcast(E4M3), rhs_scale=hid_s[h][:], start=True, stop=True,
+                )
+
+        def table_entries(h):
+            for m in range(2):
+                nc.scalar.activation(tz_g[:, h, m, :], tz_sb[:, m, :].indirect(half_list(idx5, h)), COPY)
+
+        def finish(h):
+            nc.vector.tensor_tensor(res[h][:], p_ps[h][:], tz_g[:, h], ADD)
+            nc.sync.dma_start(out_v[:, :, HALF * h : HALF * (h + 1)], res[h][:])
+
+        look_up(True, 0, 0)
+        look_up(True, 0, 1)
+        look_up(True, 0, 2)
+        look_up(False, 0, 3)
+        look_up(False, 1, 3)
+        look_up(False, 1, 2)
+        look_up(False, 1, 1)
+        larger(0)
+        look_up(True, 1, 0)
+        quantise(0)
+        table_entries(0)
+        larger(1)
+        finish(0)
+        table_entries(1)
+        quantise(1)
+        finish(1)

@@ -40,40 +40,42 @@ def tile_list_oneforboth_board_one_tabled_kernel(
         idx4 = lists.tile([P, LIST_COLS], U16, name="idx4")
         idx5 = lists.tile([P, LIST_COLS], U16, name="idx5")
 
-        xt_w = sb.tile([P, T], I32, name="xt_w", align_bytes=64)
+        xt_w = sb.tile([P, T], I32, name="xt_w", tag="xt_w", align_bytes=64)
         xt_s = sb.tile([P, T], U8, name="xt_s", align_bytes=64)
         xo_w = sb.tile([P, Z], I32, name="xo_w", align_bytes=64)
         xo_s = sb.tile([P, Z], U8, name="xo_s", align_bytes=64)
-        w_raw = sb.tile([P, 2 * R], U8, name="w_raw", align_bytes=64)
+        w_raw = sb.tile([P, 2 * R], U8, name="w_raw", tag="w_raw", align_bytes=64)
         ws_raw = sb.tile([P, R], U8, name="ws_raw", align_bytes=64)
         w_q = sb.tile([P, 2 * R], U8, name="w_q", align_bytes=64)
-        w_s = sb.tile([P, R], U8, name="w_s", align_bytes=64)
         wb_q = sb.tile([P, 2 * N], U8, name="wb_q", align_bytes=64)
         wb_s = sb.tile([P, N], U8, name="wb_s", align_bytes=64)
-        tz_sb = sb.tile([P, 2, E], F32, name="tz_sb", align_bytes=64)
-        board = [sb.tile([P, C], F32, name="board%d" % t, align_bytes=64) for t in range(PACK)]
+        board = [sb.tile([P, C], F32, name="board%d" % t, tag="board%d" % t, align_bytes=64) for t in range(PACK)]
 
         def load_rows(queue, plane, scales, q):
+            queue.dma_start(plane[32 * q : 32 * q + 4, :].bitcast(I32), scales[0, 4 * q : 4 * q + 4, :].bitcast(I32))
+
+        def load_rows_repeated(queue, plane, scales, q):
             rows = scales[0, 4 * q : 4 * q + 4, :].bitcast(I32)
             queue.dma_start(plane[32 * q : 32 * q + 32, :].bitcast(I32), rows.partition_broadcast(8))
 
+        for plane in (xo_s, wb_s):
+            nc.vector.memset(plane[:].bitcast(I32), 0)
         for t in range(PACK):
             nc.vector.memset(board[t][:], 0.0)
 
-        for q in range(4):
-            load_rows(nc.sync if q < 2 else nc.scalar, xt_s, xt_scales, q)
-        nc.sync.dma_start(xt_w[:], xt_words[0].rearrange("p n t -> p (n t)").bitcast(I32))
         nc.sync.dma_start(idx[:], offs)
-        nc.sync.dma_start(w_raw[:].bitcast(I32), w_words[0].bitcast(I32))
-        nc.sync.dma_start(xo_w[:], xo_words[0].rearrange("p n t -> p (n t)").bitcast(I32))
         for q in range(4):
-            load_rows(nc.sync, ws_raw, w_scales, q)
+            load_rows_repeated(nc.scalar if q < 2 else nc.sync, xt_s, xt_scales, q)
+        nc.scalar.dma_start(xt_w[:], xt_words[0].rearrange("p n t -> p (n t)").bitcast(I32))
+        nc.sync.dma_start(w_raw[:].bitcast(I32), w_words[0].bitcast(I32))
+        for q in range(4):
+            load_rows_repeated(nc.sync, ws_raw, w_scales, q)
+        nc.sync.dma_start(xo_w[:], xo_words[0].rearrange("p n t -> p (n t)").bitcast(I32))
         nc.sync.dma_start(idx2[:], offs2)
         nc.sync.dma_start(idx3[:], offs3)
         for q in range(4):
-            load_rows(nc.sync if q < 1 else nc.gpsimd, xo_s, xo_scales, q)
+            load_rows(nc.sync, xo_s, xo_scales, q)
         nc.sync.dma_start(idx4[:], offs4)
-        nc.sync.dma_start(tz_sb[:], tz.rearrange("(m p) e -> p m e", p=P))
         nc.sync.dma_start(wb_q[:].bitcast(I32), wb_words[0].bitcast(I32))
         for q in range(4):
             load_rows(nc.sync, wb_s, wb_scales, q)
@@ -81,36 +83,37 @@ def tile_list_oneforboth_board_one_tabled_kernel(
 
         xt_gw = sb.tile([P, J], U32, name="xt_gw", align_bytes=64)
         xt_gs = sb.tile([P, J], U8, name="xt_gs", align_bytes=64)
-        xo_gw = sb.tile([P, J], U32, name="xo_gw", align_bytes=64)
-        xo_gs = sb.tile([P, J], U8, name="xo_gs", align_bytes=64)
+        nc.vector.tensor_copy(xt_gs[:], xt_s[:].indirect(idx[:]))
         nc.vector.tensor_copy(
             w_q[:].bitcast(U16).rearrange("p (t m) -> p t m", t=PACK),
             w_raw[:].bitcast(U16).rearrange("p (m t) -> p t m", t=PACK),
         )
+        tz_sb = sb.tile([P, 2, E], F32, name="tz_sb", tag="w_raw", align_bytes=64)
+        nc.sync.dma_start(tz_sb[:], tz.rearrange("(m p) e -> p m e", p=P))
         nc.vector.tensor_copy(xt_gw[:], xt_w[:].bitcast(U32).indirect(idx[:]))
-        nc.vector.tensor_copy(xt_gs[:], xt_s[:].indirect(idx[:]))
-        nc.vector.tensor_copy(
-            w_s[:].rearrange("p (t m) -> p t m", t=PACK),
-            ws_raw[:].rearrange("p (m t) -> p t m", t=PACK),
-        )
-        nc.vector.tensor_copy(xo_gw[:], xo_w[:].bitcast(U32).indirect(idx2[:]))
-        nc.vector.tensor_copy(xo_gs[:], xo_s[:].indirect(idx2[:]))
+        w_s = sb.tile([P, R], U8, name="w_s", tag="xt_w", align_bytes=64)
+        for t in range(PACK):
+            nc.vector.tensor_copy(w_s[:, P * t : P * (t + 1)], ws_raw[:].rearrange("p (m t) -> p t m", t=PACK)[:, t, :])
 
         def w_slice(t):
             return dict(lhsT=w_q[:, 2 * P * t : 2 * P * (t + 1)].bitcast(E2M1), lhsT_scale=w_s[:, P * t : P * (t + 1)])
 
         a_ps = [ps.tile([P, J], F32, name="a_ps%d" % t) for t in range(PACK)]
-        a_sb = [sb.tile([P, J], F32, name="a_sb%d" % t, tag="stage%d" % t, align_bytes=64) for t in range(PACK)]
+        a_sb = [sb.tile([P, J], F32, name="a_sb%d" % t, align_bytes=64) for t in range(PACK)]
         for t in range(PACK):
             nc.tensor.matmul_mx(
                 out=a_ps[t][:], rhs=xt_gw[:].bitcast(E5M2), rhs_scale=xt_gs[:], start=True, stop=True, **w_slice(t)
             )
 
+        xo_gw = sb.tile([P, J], U32, name="xo_gw", align_bytes=64)
+        xo_gs = sb.tile([P, J], U8, name="xo_gs", align_bytes=64)
+        nc.vector.tensor_copy(xo_gw[:], xo_w[:].bitcast(U32).indirect(idx2[:]))
         for t in range(PACK):
             nc.scalar.activation(a_sb[t][:], a_ps[t][:], COPY)
-        for t in (0, 1):
+        for t in (0, 3):
             nc.vector.tensor_copy(board[t][:].indirect(idx3[:]), a_sb[t][:])
-        for t in (2, 3):
+        nc.vector.tensor_copy(xo_gs[:], xo_s[:].indirect(idx2[:]))
+        for t in (1, 2):
             nc.scalar.activation(board[t][:].indirect(idx3[:]), a_sb[t][:], COPY)
 
         b_ps = [ps.tile([P, PACK, HALF], F32, name="b_ps%d" % h) for h in range(2)]
@@ -124,12 +127,8 @@ def tile_list_oneforboth_board_one_tabled_kernel(
 
         read = [sb.tile([P, PACK, HALF], F32, name="read%d" % h, align_bytes=64) for h in range(2)]
         hid = [sb.tile([P, HALF, PACK], BF16, name="hid%d" % h, align_bytes=64) for h in range(2)]
-        hid_q = [sb.tile([P, HALF], U32, name="hid_q%d" % h, align_bytes=64) for h in range(2)]
-        hid_s = [sb.tile([P, HALF], U8, name="hid_s%d" % h, align_bytes=64) for h in range(2)]
-        tz_g = sb.tile([P, 2, 2, HALF], F32, name="tz_g", tag="stage3", align_bytes=64)
-        p_ps = [ps.tile([P, 2, HALF], F32, name="p_ps%d" % h) for h in range(2)]
-        res = [sb.tile([P, 2, HALF], F32, name="res%d" % h, align_bytes=64) for h in range(2)]
-        out_v = out.rearrange("(m p) j -> p m j", p=P)
+        hid_q = sb.tile([P, J], U32, name="hid_q", align_bytes=64)
+        hid_s = sb.tile([P, J], U8, name="hid_s", align_bytes=64)
 
         def half_list(lst, h):
             return lst[:, (LIST_COLS // 2) * h : (LIST_COLS // 2) * (h + 1)]
@@ -143,44 +142,38 @@ def tile_list_oneforboth_board_one_tabled_kernel(
 
         def larger(h):
             nc.vector.tensor_tensor(
-                hid[h][:].rearrange("p (c i) t -> p c t i", i=4),
-                read[h][:].rearrange("p t (c i) -> p c t i", i=4),
-                b_ps[h][:].rearrange("p t (c i) -> p c t i", i=4),
+                hid[h][:].rearrange("p (c i) t -> p c t i", i=2),
+                read[h][:].rearrange("p t (c i) -> p c t i", i=2),
+                b_ps[h][:].rearrange("p t (c i) -> p c t i", i=2),
                 MAX,
             )
 
         def quantise(h):
+            cols = slice(HALF * h, HALF * (h + 1))
             nc.vector.quantize_mx(
-                out=hid_q[h][:].bitcast(E4M3), scales=hid_s[h][:], in_=hid[h][:].rearrange("p j t -> p (j t)")
+                out=hid_q[:, cols].bitcast(E4M3), scales=hid_s[:, cols], in_=hid[h][:].rearrange("p j t -> p (j t)")
             )
-            for m in range(2):
-                nc.tensor.matmul_mx(
-                    out=p_ps[h][:, m, :],
-                    lhsT=wb_q[:, 2 * P * m : 2 * P * (m + 1)].bitcast(E2M1), lhsT_scale=wb_s[:, P * m : P * (m + 1)],
-                    rhs=hid_q[h][:].bitcast(E4M3), rhs_scale=hid_s[h][:], start=True, stop=True,
-                )
 
-        def table_entries(h):
-            for m in range(2):
-                nc.scalar.activation(tz_g[:, h, m, :], tz_sb[:, m, :].indirect(half_list(idx5, h)), COPY)
+        for t in range(PACK - 1):
+            look_up(False, 0, t)
+        look_up(True, 0, 3)
+        look_up(True, 1, 3)
+        for t in range(PACK - 1):
+            look_up(False, 1, t)
+        for h in range(2):
+            larger(h)
+        for h in range(2):
+            quantise(h)
 
-        def finish(h):
-            nc.vector.tensor_tensor(res[h][:], p_ps[h][:], tz_g[:, h], ADD)
-            nc.sync.dma_start(out_v[:, :, HALF * h : HALF * (h + 1)], res[h][:])
-
-        look_up(True, 0, 0)
-        look_up(True, 0, 1)
-        look_up(True, 0, 2)
-        look_up(False, 0, 3)
-        look_up(False, 1, 3)
-        look_up(False, 1, 2)
-        look_up(False, 1, 1)
-        larger(0)
-        look_up(True, 1, 0)
-        quantise(0)
-        table_entries(0)
-        larger(1)
-        finish(0)
-        table_entries(1)
-        quantise(1)
-        finish(1)
+        tz_g = sb.tile([P, 2, J], F32, name="tz_g", tag="board0", align_bytes=64)
+        for m in range(2):
+            p_ps = ps.tile([P, J], F32, name="p_ps%d" % m)
+            res = sb.tile([P, J], F32, name="res%d" % m, align_bytes=64)
+            nc.scalar.activation(tz_g[:, m, :], tz_sb[:, m, :].indirect(idx5[:]), COPY)
+            nc.tensor.matmul_mx(
+                out=p_ps[:], lhsT=wb_q[:, 2 * P * m : 2 * P * (m + 1)].bitcast(E2M1),
+                lhsT_scale=wb_s[:, P * m : P * (m + 1)],
+                rhs=hid_q[:].bitcast(E4M3), rhs_scale=hid_s[:], start=True, stop=True,
+            )
+            nc.vector.tensor_tensor(res[:], p_ps[:], tz_g[:, m, :], ADD)
+            nc.sync.dma_start(out[P * m : P * (m + 1), :], res[:])

@@ -154,18 +154,16 @@ def tile_list_oneforboth_board_one_tabled_kernel(
                 out=hid_q[:, cols].bitcast(E4M3), scales=hid_s[:, cols], in_=hid[h][:].rearrange("p j t -> p (j t)")
             )
 
-        for t in range(PACK - 1):
-            look_up(False, 0, t)
-        look_up(True, 0, 3)
-        look_up(True, 1, 3)
-        for t in range(PACK - 1):
-            look_up(False, 1, t)
+        for h, t in ((0, 0), (0, 1), (0, 2), (1, 1), (1, 2)):
+            look_up(False, h, t)
+        for h, t in ((0, 3), (1, 3), (1, 0)):
+            look_up(True, h, t)
         for h in range(2):
             larger(h)
         for h in range(2):
             quantise(h)
 
-        tz_g = sb.tile([P, 2, J], F32, name="tz_g", tag="board0", align_bytes=64)
+        tz_g = sb.tile([P, 2, J], F32, name="tz_g", tag="board2", align_bytes=64)
         for m in range(2):
             p_ps = ps.tile([P, J], F32, name="p_ps%d" % m)
             res = sb.tile([P, J], F32, name="res%d" % m, align_bytes=64)

from contextlib import ExitStack

import concourse.mybir as mybir

K, T, Z, J, R, C, N, E = 512, 1024, 1024, 256, 512, 512, 256, 1024
FLOPS = 2 * (2 * K * R * J + R * N * J)

F32 = mybir.dt.float32
BF16 = mybir.dt.bfloat16
I32 = mybir.dt.int32
U32 = mybir.dt.uint32
U16 = mybir.dt.uint16
U8 = mybir.dt.uint8
E4M3 = mybir.dt.float8_e4m3fn_x4
E5M2 = mybir.dt.float8_e5m2_x4
E2M1 = mybir.dt.float4_e2m1fn_x4
COPY = mybir.ActivationFunctionType.Copy
MAX = mybir.AluOpType.max
ADD = mybir.AluOpType.add

P = 128
PACK = 4
HALF = J // 2
LIST_COLS = J // 16


def tile_list_oneforboth_board_one_tabled_kernel(
    tc, xt_words, xt_scales, xo_words, xo_scales, w_words, w_scales, wb_words, wb_scales, tz,
    offs, offs2, offs3, offs4, offs5, out,
):
    nc = tc.nc
    with ExitStack() as ctx:
        lists = ctx.enter_context(tc.tile_pool(name="lists", bufs=1))
        sb = ctx.enter_context(tc.tile_pool(name="sb", bufs=1))
        ps = ctx.enter_context(tc.psum_pool(name="ps", bufs=1))

        idx = lists.tile([P, LIST_COLS], U16, name="idx")
        idx2 = lists.tile([P, LIST_COLS], U16, name="idx2")
        idx3 = lists.tile([P, LIST_COLS], U16, name="idx3")
        idx4 = lists.tile([P, LIST_COLS], U16, name="idx4")
        idx5 = lists.tile([P, LIST_COLS], U16, name="idx5")

        xt_w = sb.tile([P, T], I32, name="xt_w", tag="xt_w", align_bytes=64)
        xt_s = sb.tile([P, T], U8, name="xt_s", align_bytes=64)
        xo_w = sb.tile([P, Z], I32, name="xo_w", align_bytes=64)
        xo_s = sb.tile([P, Z], U8, name="xo_s", align_bytes=64)
        w_raw = sb.tile([P, 2 * R], U8, name="w_raw", tag="w_raw", align_bytes=64)
        ws_raw = sb.tile([P, R], U8, name="ws_raw", align_bytes=64)
        w_q = sb.tile([P, 2 * R], U8, name="w_q", align_bytes=64)
        wb_q = sb.tile([P, 2 * N], U8, name="wb_q", align_bytes=64)
        wb_s = sb.tile([P, N], U8, name="wb_s", align_bytes=64)
        board = [sb.tile([P, C], F32, name="board%d" % t, tag="board%d" % t, align_bytes=64) for t in range(PACK)]

        def load_rows(queue, plane, scales, q):
            queue.dma_start(plane[32 * q : 32 * q + 4, :].bitcast(I32), scales[0, 4 * q : 4 * q + 4, :].bitcast(I32))

        def load_rows_repeated(queue, plane, scales, q):
            rows = scales[0, 4 * q : 4 * q + 4, :].bitcast(I32)
            queue.dma_start(plane[32 * q : 32 * q + 32, :].bitcast(I32), rows.partition_broadcast(8))

        for plane in (xo_s, wb_s):
            nc.vector.memset(plane[:].bitcast(I32), 0)
        for t in range(PACK):
            nc.vector.memset(board[t][:], 0.0)

        nc.sync.dma_start(idx[:], offs)
        for q in range(4):
            load_rows_repeated(nc.scalar if q < 2 else nc.sync, xt_s, xt_scales, q)
        nc.scalar.dma_start(xt_w[:], xt_words[0].rearrange("p n t -> p (n t)").bitcast(I32))
        nc.sync.dma_start(w_raw[:].bitcast(I32), w_words[0].bitcast(I32))
        for q in range(4):
            load_rows_repeated(nc.sync, ws_raw, w_scales, q)
        nc.sync.dma_start(xo_w[:], xo_words[0].rearrange("p n t -> p (n t)").bitcast(I32))
        nc.sync.dma_start(idx2[:], offs2)
        nc.sync.dma_start(idx3[:], offs3)
        for q in range(4):
            load_rows(nc.sync, xo_s, xo_scales, q)
        nc.sync.dma_start(idx4[:], offs4)
        nc.sync.dma_start(wb_q[:].bitcast(I32), wb_words[0].bitcast(I32))
        for q in range(4):
            load_rows(nc.sync, wb_s, wb_scales, q)
        nc.sync.dma_start(idx5[:], offs5)

        xt_gw = sb.tile([P, J], U32, name="xt_gw", align_bytes=64)
        xt_gs = sb.tile([P, J], U8, name="xt_gs", align_bytes=64)
        nc.vector.tensor_copy(xt_gs[:], xt_s[:].indirect(idx[:]))
        nc.vector.tensor_copy(
            w_q[:].bitcast(U16).rearrange("p (t m) -> p t m", t=PACK),
            w_raw[:].bitcast(U16).rearrange("p (m t) -> p t m", t=PACK),
        )
        tz_sb = sb.tile([P, 2, E], F32, name="tz_sb", tag="w_raw", align_bytes=64)
        nc.sync.dma_start(tz_sb[:], tz.rearrange("(m p) e -> p m e", p=P))
        nc.vector.tensor_copy(xt_gw[:], xt_w[:].bitcast(U32).indirect(idx[:]))
        w_s = sb.tile([P, R], U8, name="w_s", tag="xt_w", align_bytes=64)
        for t in range(PACK):
            nc.vector.tensor_copy(w_s[:, P * t : P * (t + 1)], ws_raw[:].rearrange("p (m t) -> p t m", t=PACK)[:, t, :])

        def w_slice(t):
            return dict(lhsT=w_q[:, 2 * P * t : 2 * P * (t + 1)].bitcast(E2M1), lhsT_scale=w_s[:, P * t : P * (t + 1)])

        a_ps = [ps.tile([P, J], F32, name="a_ps%d" % t) for t in range(PACK)]
        a_sb = [sb.tile([P, J], F32, name="a_sb%d" % t, align_bytes=64) for t in range(PACK)]
        for t in range(PACK):
            nc.tensor.matmul_mx(
                out=a_ps[t][:], rhs=xt_gw[:].bitcast(E5M2), rhs_scale=xt_gs[:], start=True, stop=True, **w_slice(t)
            )

        xo_gw = sb.tile([P, J], U32, name="xo_gw", align_bytes=64)
        xo_gs = sb.tile([P, J], U8, name="xo_gs", align_bytes=64)
        nc.vector.tensor_copy(xo_gw[:], xo_w[:].bitcast(U32).indirect(idx2[:]))
        for t in range(PACK):
            nc.scalar.activation(a_sb[t][:], a_ps[t][:], COPY)
        for t in (0, 3):
            nc.vector.tensor_copy(board[t][:].indirect(idx3[:]), a_sb[t][:])
        nc.vector.tensor_copy(xo_gs[:], xo_s[:].indirect(idx2[:]))
        for t in (1, 2):
            nc.scalar.activation(board[t][:].indirect(idx3[:]), a_sb[t][:], COPY)

        b_ps = [ps.tile([P, PACK, HALF], F32, name="b_ps%d" % h) for h in range(2)]
        for h in range(2):
            cols = slice(HALF * h, HALF * (h + 1))
            for t in range(PACK):
                nc.tensor.matmul_mx(
                    out=b_ps[h][:, t, :], rhs=xo_gw[:, cols].bitcast(E4M3), rhs_scale=xo_gs[:, cols],
                    start=True, stop=True, **w_slice(t)
                )

        read = [sb.tile([P, PACK, HALF], F32, name="read%d" % h, align_bytes=64) for h in range(2)]
        hid = [sb.tile([P, HALF, PACK], BF16, name="hid%d" % h, align_bytes=64) for h in range(2)]
        hid_q = sb.tile([P, J], U32, name="hid_q", align_bytes=64)
        hid_s = sb.tile([P, J], U8, name="hid_s", align_bytes=64)

        def half_list(lst, h):
            return lst[:, (LIST_COLS // 2) * h : (LIST_COLS // 2) * (h + 1)]

        def look_up(on_vector, h, t):
            window = board[t][:].indirect(half_list(idx4, h))
            if on_vector:
                nc.vector.tensor_copy(read[h][:, t, :], window)
            else:
                nc.scalar.activation(read[h][:, t, :], window, COPY)

        def larger(h):
            nc.vector.tensor_tensor(
                hid[h][:].rearrange("p (c i) t -> p c t i", i=2),
                read[h][:].rearrange("p t (c i) -> p c t i", i=2),
                b_ps[h][:].rearrange("p t (c i) -> p c t i", i=2),
                MAX,
            )

        def quantise(h):
            cols = slice(HALF * h, HALF * (h + 1))
            nc.vector.quantize_mx(
                out=hid_q[:, cols].bitcast(E4M3), scales=hid_s[:, cols], in_=hid[h][:].rearrange("p j t -> p (j t)")
            )

        for h, t in ((0, 0), (0, 1), (0, 2), (1, 1), (1, 2)):
            look_up(False, h, t)
        for h, t in ((0, 3), (1, 3), (1, 0)):
            look_up(True, h, t)
        for h in range(2):
            larger(h)
        for h in range(2):
            quantise(h)

        tz_g = sb.tile([P, 2, J], F32, name="tz_g", tag="board2", align_bytes=64)
        for m in range(2):
            p_ps = ps.tile([P, J], F32, name="p_ps%d" % m)
            res = sb.tile([P, J], F32, name="res%d" % m, align_bytes=64)
            nc.scalar.activation(tz_g[:, m, :], tz_sb[:, m, :].indirect(idx5[:]), COPY)
            nc.tensor.matmul_mx(
                out=p_ps[:], lhsT=wb_q[:, 2 * P * m : 2 * P * (m + 1)].bitcast(E2M1),
                lhsT_scale=wb_s[:, P * m : P * (m + 1)],
                rhs=hid_q[:].bitcast(E4M3), rhs_scale=hid_s[:], start=True, stop=True,
            )
            nc.vector.tensor_tensor(res[:], p_ps[:], tz_g[:, m, :], ADD)
            nc.sync.dma_start(out[P * m : P * (m + 1), :], res[:])
